import numpy as np, ml_dtypes
CORES = [113,118,241,246]
N = 4
import mx_ref
NC, G = 384, 4
M = NC // N
C = np.float32(0.041)
BF = ml_dtypes.bfloat16
def cut(t, i, w=512):
    return t[:, w * i:w * i + w]
def tile(rs):
    return np.stack(rs, axis=2).reshape(128, -1).astype(BF)
def layer(w, X):
    out = []
    for i in range(G):
        for t in range(len(X)):
            p = mx_ref.matmul(mx_ref.quantize(cut(w, len(X) * i + t)), X[t])
            z = p if t == 0 else z + p
        out.append(z)
    return out
def act(Z):
    return [np.maximum(z, 0) * C for z in Z]
def setup_inputs(rng):
    def f(*shape):
        return mx_ref.flush((rng.standard_normal(shape, dtype=np.float32) * np.exp2(rng.integers(-2, 3, shape[:-1] + (1,)))).astype(BF))
    return {"x": f(N, 128, 4 * NC), "w1": f(N, 128, G * 512), "w2": f(N, 128, 512)}
def setup_inputs_blocks(rng):
    d = setup_inputs(rng)
    for k in ("x", "w1", "w2"): d[k] = mx_ref.spread(d[k], rng, 4)
    return d
def setup_inputs_wide(rng):
    d = setup_inputs(rng)
    for k in ("x", "w1", "w2"): d[k] = mx_ref.flush((d[k].astype(np.float32) * np.exp2(rng.integers(-8, 9, (N, 1, 1))).astype(np.float32)).astype(BF))
    return d
def setup_inputs_zeros(rng):
    d = setup_inputs(rng); v = d["x"].reshape(N, 128, -1, 4).copy()
    v[np.broadcast_to((rng.random((N, 1, v.shape[2], 1)) < 0.33), v.shape)] = 0
    d["x"] = v.reshape(d["x"].shape)
    return d
def reference(x, w1, w2):
    h = [tile(act(layer(w1[j], [mx_ref.quantize(x[j])]))) for j in range(N)]
    y = np.zeros((N, 128, NC), np.float32)
    for r in range(N):
        t = np.concatenate([cut(h[j], r, 4 * M) for j in range(N)], axis=1)
        y[r] = mx_ref.matmul(mx_ref.quantize(w2[r]), mx_ref.quantize(t))
    return {"y": y}

@@ -1,0 +1,178 @@
+from concourse.bass import DstId, RemoteDMATransfer
+from concourse.mybir import dt, AluOpType, ActivationFunctionType
+
+N = 4
+NC = 384
+RUN = NC // N
+HALF = 2 * RUN
+C = 0.041
+
+SCRATCH = {
+    "xt": ("sbuf", [128, 4 * NC], "bfloat16"),
+    "w1t": ("sbuf", [128, 4 * 512], "bfloat16"),
+    "w2t": ("sbuf", [128, 512], "bfloat16"),
+    "xq": ("sbuf", [128, NC], "float8_e4m3fn_x4"), "xs": ("sbuf", [128, NC], "uint8"),
+    "w1q": ("sbuf", [128, 512], "float8_e4m3fn_x4"), "w1s": ("sbuf", [128, 512], "uint8"),
+    "w2q": ("sbuf", [128, 128], "float8_e4m3fn_x4"), "w2s": ("sbuf", [128, 128], "uint8"),
+    "ht": ("sbuf", [128, 4 * NC], "bfloat16"),
+    "haq": ("sbuf", [128, HALF], "float8_e4m3fn_x4"), "has": ("sbuf", [128, HALF], "uint8"),
+    "bnq": ("sbuf", [128, 3 * RUN], "float8_e4m3fn_x4"), "bns": ("sbuf", [128, 3 * RUN], "uint8"),
+    "bfq": ("sbuf", [128, HALF], "float8_e4m3fn_x4"), "bfs": ("sbuf", [128, HALF], "uint8"),
+    "ysb": ("sbuf", [128, NC], "float32"),
+    "za": ("psum", [128, 4 * 512], "float32"),
+    "zb": ("psum", [128, 4 * 512], "float32"),
+}
+SEMAPHORES = (["ld_xa", "ld_wa", "ld_wb", "ld_xb", "ld_w2", "q_xa", "q_xb", "q_v", "act_a", "act_b", "h_a", "h_b",
+               "far", "near", "sent", "m_yn", "m_yf", "c_yn", "c_yf", "st_n", "st_f"]
+              + ["q_w%d" % i for i in range(4)] + ["m_a%d" % i for i in range(4)] + ["m_b%d" % i for i in range(4)])
+
+
+def _engines(mask):
+    return [e for e in range(mask.bit_length()) if (mask >> e) & 1]
+
+
+def _mask(engines):
+    m = 0
+    for e in engines:
+        m |= 1 << e
+    return m
+
+
+def _split(T, topo, r):
+    def place(c):
+        return (topo.host(c), topo.chip(c))
+    here = place(T.cores[r])
+    near = [j for j in range(N) if j != r and place(T.cores[j]) == here]
+    far = [j for j in range(N) if place(T.cores[j]) != here]
+    return near[0], far
+
+
+def _layout(r, peer):
+    if r < peer:
+        return {"land": 0, "quant": RUN, "out": 2 * RUN, "win": 0}
+    return {"out": 0, "quant": 0, "land": 2 * RUN, "win": RUN}
+
+
+def rank_program(g, core, T, topo):
+    me = T.rank_of(core)
+    if me is None:
+        return
+    S = T.sem
+    peer, far = _split(T, topo, me)
+    a0 = RUN * min(far)
+    b0 = RUN * min(me, peer)
+    L = _layout(me, peer)
+    relu = ActivationFunctionType.Relu
+
+    def cols(t, c0, n, k=1):
+        return t[:, k * c0:k * (c0 + n)]
+
+    g.sync.dma_start(cols(T.xt, a0, HALF, 4), cols(T.x, a0, HALF, 4)).then_inc(S.ld_xa, 16)
+    g.scalar.dma_start(T.w1t[:, 0:1024], T.w1[:, 0:1024]).then_inc(S.ld_wa, 16)
+    g.sync.dma_start(T.w1t[:, 1024:2048], T.w1[:, 1024:2048]).then_inc(S.ld_wb, 16)
+    g.scalar.dma_start(cols(T.xt, b0, HALF, 4), cols(T.x, b0, HALF, 4)).then_inc(S.ld_xb, 16)
+    g.sync.dma_start(T.w2t[:], T.w2[:]).then_inc(S.ld_w2, 16)
+
+    def q_w1(i):
+        g.vector.quantize_mx(cols(T.w1q, 128 * i, 128), cols(T.w1s, 128 * i, 128),
+                             cols(T.w1t, 128 * i, 128, 4)).then_inc(S["q_w%d" % i], 1)
+
+    def act_view(c0, b):
+        return T.ht[:, 4 * c0 + b:4 * (c0 + HALF):4]
+
+    def act_scalar(z, c0, b, done, sem):
+        g.scalar.wait_ge(done, 1)
+        g.scalar.activation(act_view(c0, b), z[:, 512 * b:512 * b + HALF], relu, scale=C).then_inc(sem, 1)
+
+    def act_vector(z, c0, b, done, sem):
+        g.vector.wait_ge(done, 1)
+        g.vector.tensor_scalar(act_view(c0, b), z[:, 512 * b:512 * b + HALF], 0.0, C,
+                               AluOpType.max, AluOpType.mult).then_inc(sem, 1)
+
+    v = g.vector
+    v.wait_ge(S.ld_xa, 16)
+    v.quantize_mx(cols(T.xq, a0, HALF), cols(T.xs, a0, HALF), cols(T.xt, a0, HALF, 4)).then_inc(S.q_xa, 1)
+    v.wait_ge(S.ld_wa, 16)
+    q_w1(0)
+    q_w1(1)
+    v.wait_ge(S.ld_wb, 16)
+    q_w1(2)
+    q_w1(3)
+    act_vector(T.za, a0, 3, S.m_a3, S.act_a)
+    v.wait_ge(S.act_a, 4)
+    v.quantize_mx(T.haq[:], T.has[:], cols(T.ht, a0, HALF, 4)).then_inc(S.h_a, 1)
+    v.wait_ge(S.ld_xb, 16)
+    v.quantize_mx(cols(T.xq, b0, HALF), cols(T.xs, b0, HALF), cols(T.xt, b0, HALF, 4)).then_inc(S.q_xb, 1)
+    act_vector(T.zb, b0, 1, S.m_b1, S.act_b)
+    act_vector(T.zb, b0, 3, S.m_b3, S.act_b)
+    v.wait_ge(S.act_b, 4)
+    v.quantize_mx(cols(T.bnq, L["quant"], HALF), cols(T.bns, L["quant"], HALF),
+                  cols(T.ht, b0, HALF, 4)).then_inc(S.h_b, 1)
+    v.wait_ge(S.ld_w2, 16)
+    v.quantize_mx(T.w2q[:], T.w2s[:], T.w2t[:]).then_inc(S.q_v, 1)
+
+    for b in (0, 1, 2):
+        act_scalar(T.za, a0, b, S["m_a%d" % b], S.act_a)
+    for b in (0, 2):
+        act_scalar(T.zb, b0, b, S["m_b%d" % b], S.act_b)
+
+    t = g.tensor
+    for z, c0, ready, name in ((T.za, a0, S.q_xa, "m_a%d"), (T.zb, b0, S.q_xb, "m_b%d")):
+        t.wait_ge(ready, 1)
+        for i in range(4):
+            if c0 == a0:
+                t.wait_ge(S["q_w%d" % i], 1)
+            t.matmul_mx(z[:, 512 * i:512 * i + HALF], cols(T.w1q, 128 * i, 128), cols(T.w1s, 128 * i, 128),
+                        cols(T.xq, c0, HALF), cols(T.xs, c0, HALF), True, True).then_inc(S[name % i], 1)
+
+    def dst_id(j):
+        rid, pid = topo.addr(T.cores[j], core)
+        return DstId(rid=rid, pnc=pid)
+
+    far_eng = _engines(topo.mask(core, T.cores[far[0]]) & topo.mask(core, T.cores[far[1]]))
+    share = len(far_eng) // len(far)
+    far_mask = [_mask(far_eng[share * k:share * (k + 1)]) for k in range(len(far))]
+    near_eng = [e for e in _engines(topo.mask(core, T.cores[peer])) if e not in far_eng]
+    near_mask = _mask(near_eng)
+    slot = _split(T, topo, far[0])[1].index(me)
+
+    g.wait_ge(S.h_a, 1)
+    g.remote_dma_fused([RemoteDMATransfer(dst_ids=[dst_id(d)], dma_engine_mask=far_mask[k], remote_sem=S.far,
+                                          src=cols(T.haq, RUN * k, RUN).bitcast(dt.uint8),
+                                          dst=cols(T.bfq, RUN * slot, RUN).bitcast(dt.uint8))
+                        for k, d in enumerate(far)], local_sem=S.sent)
+    g.remote_dma_fused([RemoteDMATransfer(dst_ids=[dst_id(d)], dma_engine_mask=far_mask[k], remote_sem=S.far,
+                                          src=cols(T.has, RUN * k, RUN), dst=cols(T.bfs, RUN * slot, RUN))
+                        for k, d in enumerate(far)], local_sem=S.sent)
+    land = _layout(peer, me)["land"]
+    rid, pid = topo.addr(T.cores[peer], core)
+    g.wait_ge(S.h_b, 1)
+    g.remote_dma(cols(T.bnq, land, RUN).bitcast(dt.uint8), cols(T.bnq, L["out"], RUN).bitcast(dt.uint8),
+                 S.near, S.sent, pid, rid, near_mask)
+    g.remote_dma(cols(T.bns, land, RUN), cols(T.bns, L["out"], RUN), S.near, S.sent, pid, rid, near_mask)
+
+    t.wait_ge(S.q_v, 1)
+    t.wait_ge(S.act_a, 4)
+    t.wait_ge(S.h_b, 1)
+    t.wait_ge(S.near, 2 * len(near_eng))
+    t.matmul_mx(T.za[:, 0:HALF], T.w2q[:], T.w2s[:], cols(T.bnq, L["win"], HALF), cols(T.bns, L["win"], HALF),
+                True, True).then_inc(S.m_yn, 1)
+    t.wait_ge(S.far, 2 * len(far) * share)
+    t.matmul_mx(T.za[:, 512:512 + HALF], T.w2q[:], T.w2s[:], T.bfq[:], T.bfs[:], True, True).then_inc(S.m_yf, 1)
+
+    order = (peer, me) if me < peer else (me, peer)
+    g.scalar.wait_ge(S.m_yn, 1)
+    for k, j in enumerate(order):
+        g.scalar.activation(cols(T.ysb, RUN * j, RUN), cols(T.za, RUN * k, RUN),
+                            ActivationFunctionType.Copy).then_inc(S.c_yn, 1)
+    g.scalar.wait_ge(S.c_yn, 2)
+    g.scalar.dma_start(cols(T.y, b0, HALF), cols(T.ysb, b0, HALF)).then_inc(S.st_n, 16)
+
+    v.wait_ge(S.m_yf, 1)
+    v.tensor_copy(cols(T.ysb, a0, HALF), T.za[:, 512:512 + HALF]).then_inc(S.c_yf, 1)
+    g.sync.wait_ge(S.c_yf, 1)
+    g.sync.dma_start(cols(T.y, a0, HALF), cols(T.ysb, a0, HALF)).then_inc(S.st_f, 16)
+
+    g.wait_ge(S.sent, 2 * len(far) * share + 2 * len(near_eng))
+    g.scalar.wait_ge(S.st_n, 16)
+    g.sync.wait_ge(S.st_f, 16)

@@ -1,30 +1,33 @@
-from concourse.bass import DstId, RemoteDMATransfer
 from concourse.mybir import dt, AluOpType, ActivationFunctionType
 
 N = 4
 NC = 384
 RUN = NC // N
 HALF = 2 * RUN
+WIN = 128
+PAD = WIN - RUN
 C = 0.041
 
 SCRATCH = {
     "xt": ("sbuf", [128, 4 * NC], "bfloat16"),
     "w1t": ("sbuf", [128, 4 * 512], "bfloat16"),
     "w2t": ("sbuf", [128, 512], "bfloat16"),
-    "xq": ("sbuf", [128, NC], "float8_e4m3fn_x4"), "xs": ("sbuf", [128, NC], "uint8"),
+    "xq": ("sbuf", [128, 4 * WIN], "float8_e4m3fn_x4"), "xs": ("sbuf", [128, 4 * WIN], "uint8"),
     "w1q": ("sbuf", [128, 512], "float8_e4m3fn_x4"), "w1s": ("sbuf", [128, 512], "uint8"),
     "w2q": ("sbuf", [128, 128], "float8_e4m3fn_x4"), "w2s": ("sbuf", [128, 128], "uint8"),
-    "ht": ("sbuf", [128, 4 * NC], "bfloat16"),
-    "haq": ("sbuf", [128, HALF], "float8_e4m3fn_x4"), "has": ("sbuf", [128, HALF], "uint8"),
-    "bnq": ("sbuf", [128, 3 * RUN], "float8_e4m3fn_x4"), "bns": ("sbuf", [128, 3 * RUN], "uint8"),
-    "bfq": ("sbuf", [128, HALF], "float8_e4m3fn_x4"), "bfs": ("sbuf", [128, HALF], "uint8"),
+    "ht": ("sbuf", [128, 4 * 4 * WIN], "bfloat16"),
+    "hoq": ("sbuf", [128, 3 * WIN], "float8_e4m3fn_x4"), "hos": ("sbuf", [128, 3 * WIN], "uint8"),
+    "p1q": ("sbuf", [128, WIN + RUN], "float8_e4m3fn_x4"), "p1s": ("sbuf", [128, WIN + RUN], "uint8"),
+    "p2q": ("sbuf", [128, HALF], "float8_e4m3fn_x4"), "p2s": ("sbuf", [128, HALF], "uint8"),
     "ysb": ("sbuf", [128, NC], "float32"),
     "za": ("psum", [128, 4 * 512], "float32"),
     "zb": ("psum", [128, 4 * 512], "float32"),
 }
-SEMAPHORES = (["ld_xa", "ld_wa", "ld_wb", "ld_xb", "ld_w2", "q_xa", "q_xb", "q_v", "act_a", "act_b", "h_a", "h_b",
-               "far", "near", "sent", "m_yn", "m_yf", "c_yn", "c_yf", "st_n", "st_f"]
-              + ["q_w%d" % i for i in range(4)] + ["m_a%d" % i for i in range(4)] + ["m_b%d" % i for i in range(4)])
+SEMAPHORES = (["ld_wa", "ld_wb", "ld_wc", "ld_w2", "q_v",
+               "early", "last", "sent", "m_y1", "m_y2", "c_y1", "c_y2a", "c_y2b", "st_a", "st_b", "st_c", "st_d"]
+              + ["ld_x%d" % k for k in range(4)] + ["q_x%d" % k for k in range(4)]
+              + ["q_w%d" % i for i in range(4)] + ["act%d" % k for k in range(4)] + ["h%d" % k for k in range(4)]
+              + ["m%d%d" % (k, i) for k in range(4) for i in range(4)])
 
 
 def _engines(mask):
@@ -44,13 +47,14 @@ def _split(T, topo, r):
     here = place(T.cores[r])
     near = [j for j in range(N) if j != r and place(T.cores[j]) == here]
     far = [j for j in range(N) if place(T.cores[j]) != here]
-    return near[0], far
+    turn = sorted(far, key=lambda j: topo.die(T.cores[j]) == topo.die(T.cores[r]))
+    return near[0], far, turn
 
 
-def _layout(r, peer):
+def _p1(r, peer):
     if r < peer:
-        return {"land": 0, "quant": RUN, "out": 2 * RUN, "win": 0}
-    return {"out": 0, "quant": 0, "land": 2 * RUN, "win": RUN}
+        return {"land": 0, "quant": RUN, "win": 0}
+    return {"quant": 0, "land": WIN, "win": PAD}
 
 
 def rank_program(g, core, T, topo):
@@ -58,121 +62,134 @@ def rank_program(g, core, T, topo):
     if me is None:
         return
     S = T.sem
-    peer, far = _split(T, topo, me)
+    peer, far, turn = _split(T, topo, me)
     a0 = RUN * min(far)
     b0 = RUN * min(me, peer)
-    L = _layout(me, peer)
-    relu = ActivationFunctionType.Relu
+    P = _p1(me, peer)
+    relu, copy = ActivationFunctionType.Relu, ActivationFunctionType.Copy
+    v, t = g.vector, g.tensor
 
-    def cols(t, c0, n, k=1):
-        return t[:, k * c0:k * (c0 + n)]
+    def cols(buf, c0, n, k=1):
+        return buf[:, k * c0:k * (c0 + n)]
 
-    g.sync.dma_start(cols(T.xt, a0, HALF, 4), cols(T.x, a0, HALF, 4)).then_inc(S.ld_xa, 16)
+    owner = [turn[0], turn[1], peer, me]
+    upper = [far.index(turn[0]), far.index(turn[1]), int(peer > me), int(me > peer)]
+    ws = [(a0 if k < 2 else b0) + (HALF - WIN) * upper[k] for k in range(4)]
+    off = [PAD * upper[k] for k in range(4)]
+    z = [T.za, T.zb, T.za, T.zb]
+    lack = [None, a0 + WIN if ws[0] == a0 else a0, None, b0 + WIN if ws[2] == b0 else b0]
+
+    g.sync.dma_start(cols(T.xt, ws[0], WIN, 4), cols(T.x, ws[0], WIN, 4)).then_inc(S.ld_x0, 16)
     g.scalar.dma_start(T.w1t[:, 0:1024], T.w1[:, 0:1024]).then_inc(S.ld_wa, 16)
-    g.sync.dma_start(T.w1t[:, 1024:2048], T.w1[:, 1024:2048]).then_inc(S.ld_wb, 16)
-    g.scalar.dma_start(cols(T.xt, b0, HALF, 4), cols(T.x, b0, HALF, 4)).then_inc(S.ld_xb, 16)
+    g.sync.dma_start(T.w1t[:, 1024:1536], T.w1[:, 1024:1536]).then_inc(S.ld_wb, 16)
+    g.sync.dma_start(T.w1t[:, 1536:2048], T.w1[:, 1536:2048]).then_inc(S.ld_wc, 16)
+    g.sync.dma_start(cols(T.xt, lack[1], HALF - WIN, 4), cols(T.x, lack[1], HALF - WIN, 4)).then_inc(S.ld_x1, 16)
+    g.sync.dma_start(cols(T.xt, ws[2], WIN, 4), cols(T.x, ws[2], WIN, 4)).then_inc(S.ld_x2, 16)
+    g.sync.dma_start(cols(T.xt, lack[3], HALF - WIN, 4), cols(T.x, lack[3], HALF - WIN, 4)).then_inc(S.ld_x3, 16)
     g.sync.dma_start(T.w2t[:], T.w2[:]).then_inc(S.ld_w2, 16)
 
     def q_w1(i):
-        g.vector.quantize_mx(cols(T.w1q, 128 * i, 128), cols(T.w1s, 128 * i, 128),
-                             cols(T.w1t, 128 * i, 128, 4)).then_inc(S["q_w%d" % i], 1)
+        v.quantize_mx(cols(T.w1q, 128 * i, 128), cols(T.w1s, 128 * i, 128),
+                      cols(T.w1t, 128 * i, 128, 4)).then_inc(S["q_w%d" % i], 1)
 
-    def act_view(c0, b):
-        return T.ht[:, 4 * c0 + b:4 * (c0 + HALF):4]
+    def q_x(k):
+        v.wait_ge(S["ld_x%d" % k], 16)
+        v.quantize_mx(cols(T.xq, WIN * k, WIN), cols(T.xs, WIN * k, WIN),
+                      cols(T.xt, ws[k], WIN, 4)).then_inc(S["q_x%d" % k], 1)
 
-    def act_scalar(z, c0, b, done, sem):
-        g.scalar.wait_ge(done, 1)
-        g.scalar.activation(act_view(c0, b), z[:, 512 * b:512 * b + HALF], relu, scale=C).then_inc(sem, 1)
+    def q_h(k, codes, plane):
+        v.wait_ge(S["act%d" % k], 4)
+        v.quantize_mx(codes, plane, cols(T.ht, WIN * k, WIN, 4)).then_inc(S["h%d" % k], 1)
 
-    def act_vector(z, c0, b, done, sem):
-        g.vector.wait_ge(done, 1)
-        g.vector.tensor_scalar(act_view(c0, b), z[:, 512 * b:512 * b + HALF], 0.0, C,
-                               AluOpType.max, AluOpType.mult).then_inc(sem, 1)
+    def act(k, b, on_vector):
+        out, in_ = T.ht[:, 4 * WIN * k + b:4 * WIN * (k + 1):4], z[k][:, 512 * b:512 * b + WIN]
+        if on_vector:
+            v.wait_ge(S["m%d%d" % (k, b)], 1)
+            v.tensor_scalar(out, in_, 0.0, C, AluOpType.max, AluOpType.mult).then_inc(S["act%d" % k], 1)
+        else:
+            g.scalar.wait_ge(S["m%d%d" % (k, b)], 1)
+            g.scalar.activation(out, in_, relu, scale=C).then_inc(S["act%d" % k], 1)
 
-    v = g.vector
-    v.wait_ge(S.ld_xa, 16)
-    v.quantize_mx(cols(T.xq, a0, HALF), cols(T.xs, a0, HALF), cols(T.xt, a0, HALF, 4)).then_inc(S.q_xa, 1)
+    def mm(k, i):
+        t.matmul_mx(z[k][:, 512 * i:512 * i + WIN], cols(T.w1q, 128 * i, 128), cols(T.w1s, 128 * i, 128),
+                    cols(T.xq, WIN * k, WIN), cols(T.xs, WIN * k, WIN), True, True).then_inc(S["m%d%d" % (k, i)], 1)
+
+    q_x(0)
     v.wait_ge(S.ld_wa, 16)
     q_w1(0)
     q_w1(1)
     v.wait_ge(S.ld_wb, 16)
     q_w1(2)
+    v.wait_ge(S.ld_wc, 16)
     q_w1(3)
-    act_vector(T.za, a0, 3, S.m_a3, S.act_a)
-    v.wait_ge(S.act_a, 4)
-    v.quantize_mx(T.haq[:], T.has[:], cols(T.ht, a0, HALF, 4)).then_inc(S.h_a, 1)
-    v.wait_ge(S.ld_xb, 16)
-    v.quantize_mx(cols(T.xq, b0, HALF), cols(T.xs, b0, HALF), cols(T.xt, b0, HALF, 4)).then_inc(S.q_xb, 1)
-    act_vector(T.zb, b0, 1, S.m_b1, S.act_b)
-    act_vector(T.zb, b0, 3, S.m_b3, S.act_b)
-    v.wait_ge(S.act_b, 4)
-    v.quantize_mx(cols(T.bnq, L["quant"], HALF), cols(T.bns, L["quant"], HALF),
-                  cols(T.ht, b0, HALF, 4)).then_inc(S.h_b, 1)
+    q_x(1)
+    q_h(0, cols(T.hoq, 0, WIN), cols(T.hos, 0, WIN))
+    q_x(2)
+    act(1, 2, True)
+    q_h(1, cols(T.hoq, WIN, WIN), cols(T.hos, WIN, WIN))
+    act(2, 1, True)
+    act(2, 3, True)
+    q_h(2, cols(T.hoq, 2 * WIN, WIN), cols(T.hos, 2 * WIN, WIN))
+    q_x(3)
+    act(3, 1, True)
+    act(3, 3, True)
+    q_h(3, cols(T.p1q, P["quant"], WIN), cols(T.p1s, P["quant"], WIN))
     v.wait_ge(S.ld_w2, 16)
     v.quantize_mx(T.w2q[:], T.w2s[:], T.w2t[:]).then_inc(S.q_v, 1)
 
-    for b in (0, 1, 2):
-        act_scalar(T.za, a0, b, S["m_a%d" % b], S.act_a)
-    for b in (0, 2):
-        act_scalar(T.zb, b0, b, S["m_b%d" % b], S.act_b)
+    for k, b in ((0, 0), (0, 1), (0, 2), (0, 3), (1, 0), (1, 1), (1, 3), (2, 0), (2, 2), (3, 0), (3, 2)):
+        act(k, b, False)
 
-    t = g.tensor
-    for z, c0, ready, name in ((T.za, a0, S.q_xa, "m_a%d"), (T.zb, b0, S.q_xb, "m_b%d")):
-        t.wait_ge(ready, 1)
+    for k in range(4):
+        t.wait_ge(S["q_x%d" % k], 1)
+        if k >= 2:
+            t.wait_ge(S["act%d" % (k - 2)], 4)
         for i in range(4):
-            if c0 == a0:
+            if k == 0:
                 t.wait_ge(S["q_w%d" % i], 1)
-            t.matmul_mx(z[:, 512 * i:512 * i + HALF], cols(T.w1q, 128 * i, 128), cols(T.w1s, 128 * i, 128),
-                        cols(T.xq, c0, HALF), cols(T.xs, c0, HALF), True, True).then_inc(S[name % i], 1)
-
-    def dst_id(j):
-        rid, pid = topo.addr(T.cores[j], core)
-        return DstId(rid=rid, pnc=pid)
+            mm(k, i)
 
     far_eng = _engines(topo.mask(core, T.cores[far[0]]) & topo.mask(core, T.cores[far[1]]))
-    share = len(far_eng) // len(far)
-    far_mask = [_mask(far_eng[share * k:share * (k + 1)]) for k in range(len(far))]
     near_eng = [e for e in _engines(topo.mask(core, T.cores[peer])) if e not in far_eng]
-    near_mask = _mask(near_eng)
-    slot = _split(T, topo, far[0])[1].index(me)
-
-    g.wait_ge(S.h_a, 1)
-    g.remote_dma_fused([RemoteDMATransfer(dst_ids=[dst_id(d)], dma_engine_mask=far_mask[k], remote_sem=S.far,
-                                          src=cols(T.haq, RUN * k, RUN).bitcast(dt.uint8),
-                                          dst=cols(T.bfq, RUN * slot, RUN).bitcast(dt.uint8))
-                        for k, d in enumerate(far)], local_sem=S.sent)
-    g.remote_dma_fused([RemoteDMATransfer(dst_ids=[dst_id(d)], dma_engine_mask=far_mask[k], remote_sem=S.far,
-                                          src=cols(T.has, RUN * k, RUN), dst=cols(T.bfs, RUN * slot, RUN))
-                        for k, d in enumerate(far)], local_sem=S.sent)
-    land = _layout(peer, me)["land"]
-    rid, pid = topo.addr(T.cores[peer], core)
-    g.wait_ge(S.h_b, 1)
-    g.remote_dma(cols(T.bnq, land, RUN).bitcast(dt.uint8), cols(T.bnq, L["out"], RUN).bitcast(dt.uint8),
-                 S.near, S.sent, pid, rid, near_mask)
-    g.remote_dma(cols(T.bns, land, RUN), cols(T.bns, L["out"], RUN), S.near, S.sent, pid, rid, near_mask)
+    d0 = turn[0]
+    ways = ((T.p1q, T.p1s, _p1(d0, _split(T, topo, d0)[0])["land"], S.early, far_eng),
+            (T.p2q, T.p2s, RUN, S.last, far_eng),
+            (T.p2q, T.p2s, 0, S.last, near_eng))
+    for k, (codes, plane, land, sem, eng) in enumerate(ways):
+        rid, pid = topo.addr(T.cores[owner[k]], core)
+        g.wait_ge(S["h%d" % k], 1)
+        g.remote_dma(cols(codes, land, RUN).bitcast(dt.uint8), cols(T.hoq, WIN * k + off[k], RUN).bitcast(dt.uint8),
+                     sem, S.sent, pid, rid, _mask(eng))
+        g.remote_dma(cols(plane, land, RUN), cols(T.hos, WIN * k + off[k], RUN), sem, S.sent, pid, rid, _mask(eng))
 
     t.wait_ge(S.q_v, 1)
-    t.wait_ge(S.act_a, 4)
-    t.wait_ge(S.h_b, 1)
-    t.wait_ge(S.near, 2 * len(near_eng))
-    t.matmul_mx(T.za[:, 0:HALF], T.w2q[:], T.w2s[:], cols(T.bnq, L["win"], HALF), cols(T.bns, L["win"], HALF),
-                True, True).then_inc(S.m_yn, 1)
-    t.wait_ge(S.far, 2 * len(far) * share)
-    t.matmul_mx(T.za[:, 512:512 + HALF], T.w2q[:], T.w2s[:], T.bfq[:], T.bfs[:], True, True).then_inc(S.m_yf, 1)
+    t.wait_ge(S.act2, 4)
+    t.wait_ge(S.h3, 1)
+    t.wait_ge(S.early, 2 * len(far_eng))
+    t.matmul_mx(T.za[:, 0:HALF], T.w2q[:], T.w2s[:], cols(T.p1q, P["win"], HALF), cols(T.p1s, P["win"], HALF),
+                True, True).then_inc(S.m_y1, 1)
+    t.wait_ge(S.last, 2 * len(far_eng) + 2 * len(near_eng))
+    t.matmul_mx(T.za[:, 512:512 + HALF], T.w2q[:], T.w2s[:], T.p2q[:], T.p2s[:], True, True).then_inc(S.m_y2, 1)
 
-    order = (peer, me) if me < peer else (me, peer)
-    g.scalar.wait_ge(S.m_yn, 1)
-    for k, j in enumerate(order):
-        g.scalar.activation(cols(T.ysb, RUN * j, RUN), cols(T.za, RUN * k, RUN),
-                            ActivationFunctionType.Copy).then_inc(S.c_yn, 1)
-    g.scalar.wait_ge(S.c_yn, 2)
-    g.scalar.dma_start(cols(T.y, b0, HALF), cols(T.ysb, b0, HALF)).then_inc(S.st_n, 16)
+    first = (turn[0], me) if me < peer else (me, turn[0])
+    g.scalar.wait_ge(S.m_y1, 1)
+    for n, j in enumerate(first):
+        g.scalar.activation(cols(T.ysb, RUN * j, RUN), cols(T.za, RUN * n, RUN), copy).then_inc(S.c_y1, 1)
+    g.scalar.wait_ge(S.c_y1, 2)
+    g.scalar.dma_start(cols(T.y, RUN * first[0], RUN), cols(T.ysb, RUN * first[0], RUN)).then_inc(S.st_a, 16)
+    g.sync.wait_ge(S.c_y1, 2)
+    g.sync.dma_start(cols(T.y, RUN * first[1], RUN), cols(T.ysb, RUN * first[1], RUN)).then_inc(S.st_b, 16)
 
-    v.wait_ge(S.m_yf, 1)
-    v.tensor_copy(cols(T.ysb, a0, HALF), T.za[:, 512:512 + HALF]).then_inc(S.c_yf, 1)
-    g.sync.wait_ge(S.c_yf, 1)
-    g.sync.dma_start(cols(T.y, a0, HALF), cols(T.ysb, a0, HALF)).then_inc(S.st_f, 16)
+    v.wait_ge(S.m_y2, 1)
+    v.tensor_copy(cols(T.ysb, RUN * peer, RUN), T.za[:, 512:512 + RUN]).then_inc(S.c_y2a, 1)
+    v.tensor_copy(cols(T.ysb, RUN * turn[1], RUN), T.za[:, 512 + RUN:512 + HALF]).then_inc(S.c_y2b, 1)
+    g.sync.wait_ge(S.c_y2a, 1)
+    g.sync.dma_start(cols(T.y, RUN * peer, RUN), cols(T.ysb, RUN * peer, RUN)).then_inc(S.st_c, 16)
+    g.scalar.wait_ge(S.c_y2b, 1)
+    g.scalar.dma_start(cols(T.y, RUN * turn[1], RUN), cols(T.ysb, RUN * turn[1], RUN)).then_inc(S.st_d, 16)
 
-    g.wait_ge(S.sent, 2 * len(far) * share + 2 * len(near_eng))
-    g.scalar.wait_ge(S.st_n, 16)
-    g.sync.wait_ge(S.st_f, 16)
+    g.wait_ge(S.sent, 4 * len(far_eng) + 2 * len(near_eng))
+    g.scalar.wait_ge(S.st_a, 16)
+    g.scalar.wait_ge(S.st_d, 16)
+    g.sync.wait_ge(S.st_b, 16)
+    g.sync.wait_ge(S.st_c, 16)

from concourse.mybir import dt, AluOpType, ActivationFunctionType

N = 4
NC = 384
RUN = NC // N
HALF = 2 * RUN
WIN = 128
PAD = WIN - RUN
C = 0.041

SCRATCH = {
    "xt": ("sbuf", [128, 4 * NC], "bfloat16"),
    "w1t": ("sbuf", [128, 4 * 512], "bfloat16"),
    "w2t": ("sbuf", [128, 512], "bfloat16"),
    "xq": ("sbuf", [128, 4 * WIN], "float8_e4m3fn_x4"), "xs": ("sbuf", [128, 4 * WIN], "uint8"),
    "w1q": ("sbuf", [128, 512], "float8_e4m3fn_x4"), "w1s": ("sbuf", [128, 512], "uint8"),
    "w2q": ("sbuf", [128, 128], "float8_e4m3fn_x4"), "w2s": ("sbuf", [128, 128], "uint8"),
    "ht": ("sbuf", [128, 4 * 4 * WIN], "bfloat16"),
    "hoq": ("sbuf", [128, 3 * WIN], "float8_e4m3fn_x4"), "hos": ("sbuf", [128, 3 * WIN], "uint8"),
    "p1q": ("sbuf", [128, WIN + RUN], "float8_e4m3fn_x4"), "p1s": ("sbuf", [128, WIN + RUN], "uint8"),
    "p2q": ("sbuf", [128, HALF], "float8_e4m3fn_x4"), "p2s": ("sbuf", [128, HALF], "uint8"),
    "ysb": ("sbuf", [128, NC], "float32"),
    "za": ("psum", [128, 4 * 512], "float32"),
    "zb": ("psum", [128, 4 * 512], "float32"),
}
SEMAPHORES = (["ld_wa", "ld_wb", "ld_wc", "ld_w2", "q_v",
               "early", "last", "sent", "m_y1", "m_y2", "c_y1", "c_y2a", "c_y2b", "st_a", "st_b", "st_c", "st_d"]
              + ["ld_x%d" % k for k in range(4)] + ["q_x%d" % k for k in range(4)]
              + ["q_w%d" % i for i in range(4)] + ["act%d" % k for k in range(4)] + ["h%d" % k for k in range(4)]
              + ["m%d%d" % (k, i) for k in range(4) for i in range(4)])


def _engines(mask):
    return [e for e in range(mask.bit_length()) if (mask >> e) & 1]


def _mask(engines):
    m = 0
    for e in engines:
        m |= 1 << e
    return m


def _split(T, topo, r):
    def place(c):
        return (topo.host(c), topo.chip(c))
    here = place(T.cores[r])
    near = [j for j in range(N) if j != r and place(T.cores[j]) == here]
    far = [j for j in range(N) if place(T.cores[j]) != here]
    turn = sorted(far, key=lambda j: topo.die(T.cores[j]) == topo.die(T.cores[r]))
    return near[0], far, turn


def _p1(r, peer):
    if r < peer:
        return {"land": 0, "quant": RUN, "win": 0}
    return {"quant": 0, "land": WIN, "win": PAD}


def rank_program(g, core, T, topo):
    me = T.rank_of(core)
    if me is None:
        return
    S = T.sem
    peer, far, turn = _split(T, topo, me)
    a0 = RUN * min(far)
    b0 = RUN * min(me, peer)
    P = _p1(me, peer)
    relu, copy = ActivationFunctionType.Relu, ActivationFunctionType.Copy
    v, t = g.vector, g.tensor

    def cols(buf, c0, n, k=1):
        return buf[:, k * c0:k * (c0 + n)]

    owner = [turn[0], turn[1], peer, me]
    upper = [far.index(turn[0]), far.index(turn[1]), int(peer > me), int(me > peer)]
    ws = [(a0 if k < 2 else b0) + (HALF - WIN) * upper[k] for k in range(4)]
    off = [PAD * upper[k] for k in range(4)]
    z = [T.za, T.zb, T.za, T.zb]
    lack = [None, a0 + WIN if ws[0] == a0 else a0, None, b0 + WIN if ws[2] == b0 else b0]

    g.sync.dma_start(cols(T.xt, ws[0], WIN, 4), cols(T.x, ws[0], WIN, 4)).then_inc(S.ld_x0, 16)
    g.scalar.dma_start(T.w1t[:, 0:1024], T.w1[:, 0:1024]).then_inc(S.ld_wa, 16)
    g.sync.dma_start(T.w1t[:, 1024:1536], T.w1[:, 1024:1536]).then_inc(S.ld_wb, 16)
    g.sync.dma_start(T.w1t[:, 1536:2048], T.w1[:, 1536:2048]).then_inc(S.ld_wc, 16)
    g.sync.dma_start(cols(T.xt, lack[1], HALF - WIN, 4), cols(T.x, lack[1], HALF - WIN, 4)).then_inc(S.ld_x1, 16)
    g.sync.dma_start(cols(T.xt, ws[2], WIN, 4), cols(T.x, ws[2], WIN, 4)).then_inc(S.ld_x2, 16)
    g.sync.dma_start(cols(T.xt, lack[3], HALF - WIN, 4), cols(T.x, lack[3], HALF - WIN, 4)).then_inc(S.ld_x3, 16)
    g.sync.dma_start(T.w2t[:], T.w2[:]).then_inc(S.ld_w2, 16)

    def q_w1(i):
        v.quantize_mx(cols(T.w1q, 128 * i, 128), cols(T.w1s, 128 * i, 128),
                      cols(T.w1t, 128 * i, 128, 4)).then_inc(S["q_w%d" % i], 1)

    def q_x(k):
        v.wait_ge(S["ld_x%d" % k], 16)
        v.quantize_mx(cols(T.xq, WIN * k, WIN), cols(T.xs, WIN * k, WIN),
                      cols(T.xt, ws[k], WIN, 4)).then_inc(S["q_x%d" % k], 1)

    def q_h(k, codes, plane):
        v.wait_ge(S["act%d" % k], 4)
        v.quantize_mx(codes, plane, cols(T.ht, WIN * k, WIN, 4)).then_inc(S["h%d" % k], 1)

    def act(k, b, on_vector):
        out, in_ = T.ht[:, 4 * WIN * k + b:4 * WIN * (k + 1):4], z[k][:, 512 * b:512 * b + WIN]
        if on_vector:
            v.wait_ge(S["m%d%d" % (k, b)], 1)
            v.tensor_scalar(out, in_, 0.0, C, AluOpType.max, AluOpType.mult).then_inc(S["act%d" % k], 1)
        else:
            g.scalar.wait_ge(S["m%d%d" % (k, b)], 1)
            g.scalar.activation(out, in_, relu, scale=C).then_inc(S["act%d" % k], 1)

    def mm(k, i):
        t.matmul_mx(z[k][:, 512 * i:512 * i + WIN], cols(T.w1q, 128 * i, 128), cols(T.w1s, 128 * i, 128),
                    cols(T.xq, WIN * k, WIN), cols(T.xs, WIN * k, WIN), True, True).then_inc(S["m%d%d" % (k, i)], 1)

    q_x(0)
    v.wait_ge(S.ld_wa, 16)
    q_w1(0)
    q_w1(1)
    v.wait_ge(S.ld_wb, 16)
    q_w1(2)
    v.wait_ge(S.ld_wc, 16)
    q_w1(3)
    q_x(1)
    q_h(0, cols(T.hoq, 0, WIN), cols(T.hos, 0, WIN))
    q_x(2)
    act(1, 2, True)
    q_h(1, cols(T.hoq, WIN, WIN), cols(T.hos, WIN, WIN))
    act(2, 1, True)
    act(2, 3, True)
    q_h(2, cols(T.hoq, 2 * WIN, WIN), cols(T.hos, 2 * WIN, WIN))
    q_x(3)
    act(3, 1, True)
    act(3, 3, True)
    q_h(3, cols(T.p1q, P["quant"], WIN), cols(T.p1s, P["quant"], WIN))
    v.wait_ge(S.ld_w2, 16)
    v.quantize_mx(T.w2q[:], T.w2s[:], T.w2t[:]).then_inc(S.q_v, 1)

    for k, b in ((0, 0), (0, 1), (0, 2), (0, 3), (1, 0), (1, 1), (1, 3), (2, 0), (2, 2), (3, 0), (3, 2)):
        act(k, b, False)

    for k in range(4):
        t.wait_ge(S["q_x%d" % k], 1)
        if k >= 2:
            t.wait_ge(S["act%d" % (k - 2)], 4)
        for i in range(4):
            if k == 0:
                t.wait_ge(S["q_w%d" % i], 1)
            mm(k, i)

    far_eng = _engines(topo.mask(core, T.cores[far[0]]) & topo.mask(core, T.cores[far[1]]))
    near_eng = [e for e in _engines(topo.mask(core, T.cores[peer])) if e not in far_eng]
    d0 = turn[0]
    ways = ((T.p1q, T.p1s, _p1(d0, _split(T, topo, d0)[0])["land"], S.early, far_eng),
            (T.p2q, T.p2s, RUN, S.last, far_eng),
            (T.p2q, T.p2s, 0, S.last, near_eng))
    for k, (codes, plane, land, sem, eng) in enumerate(ways):
        rid, pid = topo.addr(T.cores[owner[k]], core)
        g.wait_ge(S["h%d" % k], 1)
        g.remote_dma(cols(codes, land, RUN).bitcast(dt.uint8), cols(T.hoq, WIN * k + off[k], RUN).bitcast(dt.uint8),
                     sem, S.sent, pid, rid, _mask(eng))
        g.remote_dma(cols(plane, land, RUN), cols(T.hos, WIN * k + off[k], RUN), sem, S.sent, pid, rid, _mask(eng))

    t.wait_ge(S.q_v, 1)
    t.wait_ge(S.act2, 4)
    t.wait_ge(S.h3, 1)
    t.wait_ge(S.early, 2 * len(far_eng))
    t.matmul_mx(T.za[:, 0:HALF], T.w2q[:], T.w2s[:], cols(T.p1q, P["win"], HALF), cols(T.p1s, P["win"], HALF),
                True, True).then_inc(S.m_y1, 1)
    t.wait_ge(S.last, 2 * len(far_eng) + 2 * len(near_eng))
    t.matmul_mx(T.za[:, 512:512 + HALF], T.w2q[:], T.w2s[:], T.p2q[:], T.p2s[:], True, True).then_inc(S.m_y2, 1)

    first = (turn[0], me) if me < peer else (me, turn[0])
    g.scalar.wait_ge(S.m_y1, 1)
    for n, j in enumerate(first):
        g.scalar.activation(cols(T.ysb, RUN * j, RUN), cols(T.za, RUN * n, RUN), copy).then_inc(S.c_y1, 1)
    g.scalar.wait_ge(S.c_y1, 2)
    g.scalar.dma_start(cols(T.y, RUN * first[0], RUN), cols(T.ysb, RUN * first[0], RUN)).then_inc(S.st_a, 16)
    g.sync.wait_ge(S.c_y1, 2)
    g.sync.dma_start(cols(T.y, RUN * first[1], RUN), cols(T.ysb, RUN * first[1], RUN)).then_inc(S.st_b, 16)

    v.wait_ge(S.m_y2, 1)
    v.tensor_copy(cols(T.ysb, RUN * peer, RUN), T.za[:, 512:512 + RUN]).then_inc(S.c_y2a, 1)
    v.tensor_copy(cols(T.ysb, RUN * turn[1], RUN), T.za[:, 512 + RUN:512 + HALF]).then_inc(S.c_y2b, 1)
    g.sync.wait_ge(S.c_y2a, 1)
    g.sync.dma_start(cols(T.y, RUN * peer, RUN), cols(T.ysb, RUN * peer, RUN)).then_inc(S.st_c, 16)
    g.scalar.wait_ge(S.c_y2b, 1)
    g.scalar.dma_start(cols(T.y, RUN * turn[1], RUN), cols(T.ysb, RUN * turn[1], RUN)).then_inc(S.st_d, 16)

    g.wait_ge(S.sent, 4 * len(far_eng) + 2 * len(near_eng))
    g.scalar.wait_ge(S.st_a, 16)
    g.scalar.wait_ge(S.st_d, 16)
    g.sync.wait_ge(S.st_b, 16)
    g.sync.wait_ge(S.st_c, 16)
